import numpy as np
import ml_dtypes


def mxq(x, axis, fmt="e4m3"):
    dtype, down = {"e4m3": (ml_dtypes.float8_e4m3fn, 7), "e5m2": (ml_dtypes.float8_e5m2, 14)}[fmt]
    v = np.moveaxis(np.asarray(x, np.float32).astype(ml_dtypes.bfloat16).astype(np.float64), axis, -1)
    blocks = v.reshape(v.shape[:-1] + (-1, 32))
    amax = np.abs(blocks).max(-1, keepdims=True)
    byte = np.maximum(np.where(amax > 0, np.frexp(amax)[1] - 1 + 127, 0) - down, 1)
    scale = np.exp2(byte - 127.0)
    codes = (blocks / scale).astype(np.float32).astype(dtype).astype(np.float64)
    return np.moveaxis((codes * scale).reshape(v.shape), -1, axis)


WIDE = False


def mx_kscale(k):
    if not WIDE:
        return np.ones(k)
    levels = np.array([10, -10, 5, -5, 0])
    if k % 512:
        return np.exp2(np.random.permutation(np.resize(levels, k // 32))).repeat(32)
    a = np.empty((k // 512, 16))
    for p in range(k // 512):
        a[p, :8] = np.random.permutation(np.resize(levels, 8))
        for g in range(8):
            far = levels[np.abs(levels - a[p, g]) >= 10]
            a[p, g + 8] = far[np.random.randint(len(far))]
    return np.exp2(a.ravel()).repeat(32)


BF16 = ml_dtypes.bfloat16


def bf(x):
    return np.asarray(x, np.float32).astype(BF16)


def f64(x):
    return np.asarray(x).astype(np.float64)


E2M1 = np.array([0.0, 0.5, 1.0, 1.5, 2.0, 3.0, 4.0, 6.0, -0.0, -0.5, -1.0, -1.5, -2.0, -3.0, -4.0, -6.0])


def pack_weight(w, fmt):
    k, n = w.shape
    w = f64(bf(w)).reshape(k // 32, 32, n)
    amax = np.abs(w).max(1)
    if fmt == "e4m3":
        byte = np.frexp(amax)[1] - 1 + 127 - 7
    else:
        mant, ex = np.frexp(amax / 6.0)
        byte = np.where(mant > 0.5, ex, ex - 1) + 127
    byte = np.clip(np.where(amax > 0, byte, 1), 1, 254)
    scaled = (w * np.exp2(127.0 - byte)[:, None, :]).reshape(k, n).astype(np.float32)
    by_word = np.ascontiguousarray(scaled.reshape(k // 512, 128, 4, n).transpose(0, 1, 3, 2))
    if fmt == "e4m3":
        words = by_word.astype(ml_dtypes.float8_e4m3fn).view(np.uint8)
    else:
        c = by_word.astype(ml_dtypes.float4_e2m1fn).view(np.uint8) & 0xF
        words = c[..., 0::2] | (c[..., 1::2] << 4)
    return np.ascontiguousarray(words), np.ascontiguousarray(byte.astype(np.uint8).reshape(k // 512, 16, n))


def unpack_weight(words, scales, fmt):
    g, p, n, _ = words.shape
    if fmt == "e4m3":
        vals = np.ascontiguousarray(words).view(ml_dtypes.float8_e4m3fn).astype(np.float64)
    else:
        nib = np.empty((g, p, n, 4), np.uint8)
        nib[..., 0::2] = words & 0xF
        nib[..., 1::2] = words >> 4
        vals = E2M1[nib]
    vals = vals * np.repeat(np.exp2(scales.astype(np.float64) - 127.0), 8, axis=1)[..., None]
    return vals.transpose(0, 1, 3, 2).reshape(g * 512, n)
def pack4(w):
    words, scales = pack_weight(w, "e2m1")
    return words.reshape(words.shape[0], 128, -1), scales


def unpack4(words, scales):
    return unpack_weight(words.reshape(words.shape[0], 128, -1, 2), scales, "e2m1")


M, K, N = 2048, 1024, 512


def setup_inputs():
    s = mx_kscale(K)
    z = np.random.standard_normal((M, K))
    total = np.maximum(z, 0.0).sum(axis=1, keepdims=True)
    lib = 0.56 * np.sqrt(K)
    d = lib * np.random.standard_normal((K, N)) / s[:, None]
    e = lib * np.random.standard_normal((K, N)) / s[:, None]
    c = (1.0 + 0.5 * lib * np.random.standard_normal((K, N))) / s[:, None]
    d_words, d_scales = pack4(d)
    e_words, e_scales = pack_weight(e, "e4m3")
    return {"z": bf(z * s),
            "inv_sum": bf(1.0 / total),
            "y": bf(np.random.standard_normal((M, N))),
            "shade": bf(0.7 * np.random.standard_normal((M, 1))),
            "d_words": d_words, "d_scales": d_scales,
            "e_words": e_words, "e_scales": e_scales,
            "c": bf(c)}


def reference(z, inv_sum, y, shade, d_words, d_scales, e_words, e_scales, c):
    a = mxq(np.maximum(f64(z), 0.0) * f64(inv_sum), 1, "e4m3")
    var = a @ unpack4(d_words, d_scales)
    mean = a @ unpack_weight(e_words, e_scales, "e4m3")
    weight = a @ mxq(f64(c), 0, "e4m3")
    return (f64(y) - mean - f64(shade) * var) * weight

@@ -1,0 +1,281 @@
+from contextlib import ExitStack
+
+import concourse.mybir as mybir
+from concourse.masks import make_identity
+
+M, K, N = 2048, 1024, 512
+P = 128
+TILES = M // P
+PASSES = K // 512
+
+FLOPS = 3 * 2 * M * K * N
+
+F32 = mybir.dt.float32
+BF16 = mybir.dt.bfloat16
+I32 = mybir.dt.int32
+U32 = mybir.dt.uint32
+U8 = mybir.dt.uint8
+E4M3X4 = mybir.dt.float8_e4m3fn_x4
+E2M1X4 = mybir.dt.float4_e2m1fn_x4
+ALU = mybir.AluOpType
+ACT = mybir.ActivationFunctionType
+
+C_SPLIT = 320
+
+
+def tile_unmixing_residual_s10_kernel(tc, z, inv_sum, y, shade, d_words, d_scales, e_words, e_scales, c, out):
+    nc = tc.nc
+    z_rows = z.rearrange("(p i) k -> p i k", i=TILES)
+    y_rows = y.rearrange("(p i) n -> p i n", i=TILES)
+    out_rows = out.rearrange("(p i) n -> p i n", i=TILES)
+    c_rows = c.rearrange("(g p j) n -> g p j n", p=P, j=4)
+
+    with ExitStack() as ctx:
+        keep = ctx.enter_context(tc.tile_pool(name="keep", bufs=1))
+        work = ctx.enter_context(tc.tile_pool(name="work", bufs=4))
+        psum = ctx.enter_context(tc.psum_pool(name="psum", bufs=2))
+
+        z_sb = keep.tile([P, TILES, K], BF16, name="z_sb", align_bytes=64)
+        y_sb = keep.tile([P, TILES, N], BF16, name="y_sb", align_bytes=64)
+        inv_bf = keep.tile([P, TILES], BF16, name="inv_bf")
+        shade_bf = keep.tile([P, TILES], BF16, name="shade_bf")
+        inv_col = keep.tile([P, TILES], F32, name="inv_col")
+        neg_shade = keep.tile([P, TILES], F32, name="neg_shade")
+        ident = keep.tile([P, P], F32, name="ident")
+        warm = keep.tile([P, 16], F32, name="warm")
+        d_codes = keep.tile([P, PASSES, 2 * N], U8, name="d_codes", align_bytes=64)
+        e_codes = keep.tile([P, PASSES, N], U32, name="e_codes", align_bytes=64)
+        c_codes = keep.tile([P, PASSES, N], U32, name="c_codes", align_bytes=64)
+        d_plane = keep.tile([P, PASSES, N], U8, name="d_plane", align_bytes=64)
+        e_plane = keep.tile([P, PASSES, N], U8, name="e_plane", align_bytes=64)
+        c_plane = keep.tile([P, PASSES, N], U8, name="c_plane", align_bytes=64)
+        c_raw = keep.tile([P, PASSES, 4, N], BF16, name="c_raw", align_bytes=64)
+        c_grouped = keep.tile([P, PASSES, N, 4], BF16, name="c_grouped", align_bytes=64)
+
+        ctx.enter_context(tc.manual_schedule())
+
+        def load_z(first, count):
+            nc.sync.dma_start(out=z_sb[:, first:first + count, :], in_=z_rows[:, first:first + count, :])
+
+        def load_y(first, count):
+            nc.sync.dma_start(out=y_sb[:, first:first + count, :], in_=y_rows[:, first:first + count, :])
+
+        def load_scales(engine, plane, scales):
+            words = scales.bitcast(I32).rearrange("g (q r) n -> r q g n", r=4)
+            for r in range(4):
+                engine.dma_start(out=plane[r:P:32, :, :].bitcast(I32), in_=words[r])
+
+        nc.vector.memset(d_plane[:].rearrange("p g n -> p (g n)").bitcast(I32), 0)
+        nc.vector.memset(e_plane[:].rearrange("p g n -> p (g n)").bitcast(I32), 0)
+        nc.vector.memset(warm[:], 0.0)
+        nc.gpsimd.dma_start(out=inv_bf[:], in_=inv_sum.rearrange("(p i) o -> p (i o)", i=TILES))
+        load_z(0, 1)
+        load_scales(nc.scalar, d_plane, d_scales)
+        nc.sync.dma_start(out=d_codes[:].bitcast(I32), in_=d_words.bitcast(I32).rearrange("g p w -> p g w"))
+        load_z(1, 1)
+        make_identity(nc, ident[:])
+        nc.gpsimd.dma_start(out=shade_bf[:], in_=shade.rearrange("(p i) o -> p (i o)", i=TILES))
+        nc.sync.dma_start(
+            out=e_codes[:].bitcast(I32),
+            in_=e_words.rearrange("g p n t -> g p (n t)").bitcast(I32).rearrange("g p w -> p g w"),
+        )
+        load_scales(nc.scalar, e_plane, e_scales)
+        load_z(2, 2)
+        load_y(0, 2)
+        for g in range(PASSES):
+            nc.sync.dma_start(out=c_raw[:, g, :, :], in_=c_rows[g])
+        load_z(4, 2)
+        load_y(2, 2)
+        load_z(6, 2)
+        load_y(4, 4)
+        for first in range(8, TILES, 4):
+            load_z(first, 2)
+            load_y(first, 4)
+            load_z(first + 2, 2)
+
+        nc.scalar.activation(out=warm[:, 0:1], in_=warm[:, 1:2], func=ACT.Relu)
+
+        a, grouped, codes, planes, xt = {}, {}, {}, {}, {}
+        var, mean, weight, t1, t2, res = {}, {}, {}, {}, {}, {}
+
+        def relu_scale(i, engine):
+            act = work.tile([P, K], BF16, name="act", align_bytes=64)
+            src = z_sb[:, i, :].rearrange("p (q u e) -> p u q e", u=2, e=2)
+            dst = act[:].rearrange("p (u q e) -> p u q e", u=2, e=2)
+            if engine == "v":
+                nc.vector.tensor_scalar(out=dst, in0=src, scalar1=0.0, scalar2=inv_col[:, i:i + 1], op0=ALU.max, op1=ALU.mult)
+            else:
+                nc.scalar.activation(out=dst, in_=src, func=ACT.Relu, scale=inv_col[:, i:i + 1])
+            a[i] = act
+
+        def transpose(i):
+            turned = psum.tile([P, 2, 2 * P], F32, name="turned")
+            words = a[i][:].bitcast(F32)
+            for b in range(4):
+                nc.tensor.transpose(turned[:, b // 2, (b % 2) * P:(b % 2 + 1) * P], words[:, b * P:(b + 1) * P], ident[:])
+            xt[i] = turned
+
+        def group(i, engine):
+            grp = work.tile([P, K], BF16, name="grp", align_bytes=64)
+            dst = grp[:].bitcast(F32).rearrange("p (x u) -> p x u", u=2)
+            src = xt[i][:].rearrange("p u x -> p x u")
+            if engine == "v":
+                nc.vector.tensor_copy(out=dst, in_=src)
+            else:
+                nc.scalar.copy(out=dst, in_=src)
+            grouped[i] = grp
+
+        def quantize(i):
+            code = work.tile([P, PASSES * P], U32, name="code", align_bytes=64)
+            plane = work.tile([P, PASSES * P], U8, name="plane", align_bytes=64)
+            nc.vector.quantize_mx(out=code[:].bitcast(E4M3X4), scales=plane[:], in_=grouped[i][:])
+            codes[i], planes[i] = code, plane
+
+        def product(i, acc, rhs, rhs_plane):
+            for g in range(PASSES):
+                cols = slice(g * P, (g + 1) * P)
+                nc.tensor.matmul_mx(
+                    out=acc[:],
+                    lhsT=codes[i][:, cols].bitcast(E4M3X4),
+                    lhsT_scale=planes[i][:, cols],
+                    rhs=rhs(g),
+                    rhs_scale=rhs_plane[:, g, :],
+                    start=(g == 0),
+                    stop=(g == PASSES - 1),
+                )
+
+        def mm_var(i):
+            var_ps = psum.tile([P, N], F32, name="var_ps")
+            product(i, var_ps, lambda g: d_codes[:, g, :].bitcast(E2M1X4), d_plane)
+            var[i] = var_ps
+
+        def mm_mean(i):
+            mean_ps = psum.tile([P, N], F32, name="mean_ps")
+            product(i, mean_ps, lambda g: e_codes[:, g, :].bitcast(E4M3X4), e_plane)
+            mean[i] = mean_ps
+
+        def mm_weight(i):
+            weight_ps = psum.tile([P, N], F32, name="weight_ps")
+            product(i, weight_ps, lambda g: c_codes[:, g, :].bitcast(E4M3X4), c_plane)
+            weight[i] = weight_ps
+
+        def ep1(i):
+            part = work.tile([P, N], F32, name="part")
+            nc.vector.scalar_tensor_tensor(
+                out=part[:], in0=var[i][:], scalar=neg_shade[:, i:i + 1], in1=y_sb[:, i, :], op0=ALU.mult, op1=ALU.add)
+            t1[i] = part
+
+        def ep2(i):
+            resid = work.tile([P, N], F32, name="resid")
+            nc.vector.tensor_tensor(out=resid[:], in0=t1[i][:], in1=mean[i][:], op=ALU.subtract)
+            t2[i] = resid
+
+        def ep3(i):
+            if i % 2 == 0:
+                pair = work.tile([P, 2, N], F32, name="pair")
+                res[i // 2] = pair
+            dst = res[i // 2]
+            nc.vector.tensor_tensor(out=dst[:, i % 2, :], in0=t2[i][:], in1=weight[i][:], op=ALU.mult)
+            if i >= TILES - 2:
+                nc.sync.dma_start(out=out_rows[:, i, :], in_=dst[:, i % 2, :])
+            elif i % 2 == 1:
+                nc.sync.dma_start(out=out_rows[:, i - 1:i + 1, :], in_=dst[:])
+
+        def c_group(g, engine):
+            cols = slice(0, C_SPLIT) if engine == "v" else slice(C_SPLIT, N)
+            src = c_raw[:, g, :, cols].rearrange("p j n -> p n j")
+            dst = c_grouped[:, g, cols, :]
+            if engine == "v":
+                nc.vector.tensor_copy(out=dst, in_=src)
+            else:
+                nc.scalar.copy(out=dst, in_=src)
+
+        def c_quantize(g):
+            nc.vector.quantize_mx(
+                out=c_codes[:, g, :].bitcast(E4M3X4), scales=c_plane[:, g, :], in_=c_grouped[:, g, :, :].rearrange("p n j -> p (n j)"))
+
+        nc.vector.tensor_copy(out=inv_col[:], in_=inv_bf[:])
+        relu_scale(0, "v")
+        relu_scale(1, "v")
+        transpose(0)
+        transpose(1)
+        group(0, "s")
+        group(1, "v")
+        quantize(0)
+        quantize(1)
+        nc.vector.tensor_scalar(out=neg_shade[:], in0=shade_bf[:], scalar1=-1.0, scalar2=None, op0=ALU.mult)
+        relu_scale(2, "v")
+        relu_scale(3, "s")
+        mm_var(0)
+        mm_mean(0)
+        transpose(2)
+        transpose(3)
+        ep1(0)
+        group(2, "s")
+        group(3, "s")
+        mm_var(1)
+        mm_mean(1)
+        ep2(0)
+        quantize(2)
+        ep1(1)
+        quantize(3)
+        c_group(0, "s")
+        c_group(1, "s")
+        c_group(0, "v")
+        c_quantize(0)
+        relu_scale(4, "s")
+        relu_scale(5, "v")
+        mm_var(2)
+        mm_mean(2)
+        ep2(1)
+        transpose(4)
+        transpose(5)
+        ep1(2)
+        c_group(1, "v")
+        c_quantize(1)
+        ep2(2)
+        group(4, "s")
+        group(5, "s")
+        relu_scale(6, "s")
+        relu_scale(7, "s")
+        mm_var(3)
+        mm_mean(3)
+        ep1(3)
+        quantize(4)
+        for i in range(4):
+            mm_weight(i)
+        ep3(0)
+        quantize(5)
+        ep2(3)
+        ep3(1)
+        ep3(2)
+        for s in range(2, TILES // 2):
+            i, j = 2 * s, 2 * s + 1
+            more = j + 2 < TILES
+            mm_var(i)
+            mm_mean(i)
+            if more:
+                transpose(i + 2)
+                transpose(j + 2)
+            mm_var(j)
+            mm_mean(j)
+            if j + 4 < TILES:
+                relu_scale(i + 4, "s")
+            if more:
+                group(i + 2, "s")
+                group(j + 2, "s")
+            if j + 4 < TILES:
+                relu_scale(j + 4, "s")
+            ep1(i)
+            ep3(i - 1)
+            ep2(i)
+            if more:
+                quantize(i + 2)
+            ep1(j)
+            if more:
+                quantize(j + 2)
+            ep2(j)
+            mm_weight(i)
+            mm_weight(j)
+            ep3(i)
+        ep3(TILES - 1)

@@ -20,7 +20,7 @@ E2M1X4 = mybir.dt.float4_e2m1fn_x4
 ALU = mybir.AluOpType
 ACT = mybir.ActivationFunctionType
 
-C_SPLIT = 320
+C_SPLIT = 256
 
 
 def tile_unmixing_residual_s10_kernel(tc, z, inv_sum, y, shade, d_words, d_scales, e_words, e_scales, c, out):
@@ -65,25 +65,34 @@ def tile_unmixing_residual_s10_kernel(tc, z, inv_sum, y, shade, d_words, d_scale
             for r in range(4):
                 engine.dma_start(out=plane[r:P:32, :, :].bitcast(I32), in_=words[r])
 
+        def load_d():
+            nc.sync.dma_start(out=d_codes[:].bitcast(I32), in_=d_words.bitcast(I32).rearrange("g p w -> p g w"))
+
+        def load_e():
+            nc.sync.dma_start(
+                out=e_codes[:].bitcast(I32),
+                in_=e_words.rearrange("g p n t -> g p (n t)").bitcast(I32).rearrange("g p w -> p g w"),
+            )
+
+        def load_c(g):
+            nc.sync.dma_start(out=c_raw[:, g, :, :], in_=c_rows[g])
+
         nc.vector.memset(d_plane[:].rearrange("p g n -> p (g n)").bitcast(I32), 0)
         nc.vector.memset(e_plane[:].rearrange("p g n -> p (g n)").bitcast(I32), 0)
         nc.vector.memset(warm[:], 0.0)
-        nc.gpsimd.dma_start(out=inv_bf[:], in_=inv_sum.rearrange("(p i) o -> p (i o)", i=TILES))
-        load_z(0, 1)
-        load_scales(nc.scalar, d_plane, d_scales)
-        nc.sync.dma_start(out=d_codes[:].bitcast(I32), in_=d_words.bitcast(I32).rearrange("g p w -> p g w"))
-        load_z(1, 1)
         make_identity(nc, ident[:])
         nc.gpsimd.dma_start(out=shade_bf[:], in_=shade.rearrange("(p i) o -> p (i o)", i=TILES))
-        nc.sync.dma_start(
-            out=e_codes[:].bitcast(I32),
-            in_=e_words.rearrange("g p n t -> g p (n t)").bitcast(I32).rearrange("g p w -> p g w"),
-        )
-        load_scales(nc.scalar, e_plane, e_scales)
+        load_z(0, 1)
+        nc.sync.dma_start(out=inv_bf[:], in_=inv_sum.rearrange("(p i) o -> p (i o)", i=TILES))
+        load_scales(nc.sync, d_plane, d_scales)
+        load_d()
+        load_z(1, 1)
+        load_e()
+        load_scales(nc.sync, e_plane, e_scales)
         load_z(2, 2)
         load_y(0, 2)
-        for g in range(PASSES):
-            nc.sync.dma_start(out=c_raw[:, g, :, :], in_=c_rows[g])
+        load_c(0)
+        load_c(1)
         load_z(4, 2)
         load_y(2, 2)
         load_z(6, 2)
@@ -92,7 +101,6 @@ def tile_unmixing_residual_s10_kernel(tc, z, inv_sum, y, shade, d_words, d_scale
             load_z(first, 2)
             load_y(first, 4)
             load_z(first + 2, 2)
-
         nc.scalar.activation(out=warm[:, 0:1], in_=warm[:, 1:2], func=ACT.Relu)
 
         a, grouped, codes, planes, xt = {}, {}, {}, {}, {}
@@ -103,7 +111,7 @@ def tile_unmixing_residual_s10_kernel(tc, z, inv_sum, y, shade, d_words, d_scale
             src = z_sb[:, i, :].rearrange("p (q u e) -> p u q e", u=2, e=2)
             dst = act[:].rearrange("p (u q e) -> p u q e", u=2, e=2)
             if engine == "v":
-                nc.vector.tensor_scalar(out=dst, in0=src, scalar1=0.0, scalar2=inv_col[:, i:i + 1], op0=ALU.max, op1=ALU.mult)
+                nc.vector.tensor_scalar(out=dst, in0=src, scalar1=0.0, scalar2=inv_bf[:, i:i + 1], op0=ALU.max, op1=ALU.mult)
             else:
                 nc.scalar.activation(out=dst, in_=src, func=ACT.Relu, scale=inv_col[:, i:i + 1])
             a[i] = act
@@ -170,12 +178,17 @@ def tile_unmixing_residual_s10_kernel(tc, z, inv_sum, y, shade, d_words, d_scale
             nc.vector.tensor_tensor(out=resid[:], in0=t1[i][:], in1=mean[i][:], op=ALU.subtract)
             t2[i] = resid
 
-        def ep3(i):
+        def w_copy(i):
+            weight_sb = work.tile([P, N], F32, name="weight_sb")
+            nc.scalar.copy(out=weight_sb[:], in_=weight[i][:])
+            weight[i] = weight_sb
+
+        def ep3(i, engine="v"):
             if i % 2 == 0:
                 pair = work.tile([P, 2, N], F32, name="pair")
                 res[i // 2] = pair
             dst = res[i // 2]
-            nc.vector.tensor_tensor(out=dst[:, i % 2, :], in0=t2[i][:], in1=weight[i][:], op=ALU.mult)
+            (nc.gpsimd if engine == "g" else nc.vector).tensor_tensor(out=dst[:, i % 2, :], in0=t2[i][:], in1=weight[i][:], op=ALU.mult)
             if i >= TILES - 2:
                 nc.sync.dma_start(out=out_rows[:, i, :], in_=dst[:, i % 2, :])
             elif i % 2 == 1:
@@ -194,61 +207,63 @@ def tile_unmixing_residual_s10_kernel(tc, z, inv_sum, y, shade, d_words, d_scale
             nc.vector.quantize_mx(
                 out=c_codes[:, g, :].bitcast(E4M3X4), scales=c_plane[:, g, :], in_=c_grouped[:, g, :, :].rearrange("p n j -> p (n j)"))
 
-        nc.vector.tensor_copy(out=inv_col[:], in_=inv_bf[:])
         relu_scale(0, "v")
+        nc.vector.tensor_copy(out=inv_col[:], in_=inv_bf[:])
         relu_scale(1, "v")
         transpose(0)
         transpose(1)
         group(0, "s")
-        group(1, "v")
         quantize(0)
+        group(1, "s")
         quantize(1)
         nc.vector.tensor_scalar(out=neg_shade[:], in0=shade_bf[:], scalar1=-1.0, scalar2=None, op0=ALU.mult)
         relu_scale(2, "v")
-        relu_scale(3, "s")
+        relu_scale(3, "v")
         mm_var(0)
         mm_mean(0)
         transpose(2)
         transpose(3)
-        ep1(0)
-        group(2, "s")
-        group(3, "s")
         mm_var(1)
         mm_mean(1)
-        ep2(0)
+        group(2, "s")
+        group(3, "s")
+        ep1(0)
         quantize(2)
-        ep1(1)
+        ep2(0)
         quantize(3)
+        ep1(1)
         c_group(0, "s")
         c_group(1, "s")
         c_group(0, "v")
-        c_quantize(0)
-        relu_scale(4, "s")
+        ep2(1)
+        relu_scale(4, "v")
         relu_scale(5, "v")
+        c_group(1, "v")
+        c_quantize(0)
+        c_quantize(1)
         mm_var(2)
         mm_mean(2)
-        ep2(1)
+        mm_var(3)
+        mm_mean(3)
         transpose(4)
         transpose(5)
+        for i in range(4):
+            mm_weight(i)
         ep1(2)
-        c_group(1, "v")
-        c_quantize(1)
-        ep2(2)
         group(4, "s")
         group(5, "s")
         relu_scale(6, "s")
         relu_scale(7, "s")
-        mm_var(3)
-        mm_mean(3)
-        ep1(3)
         quantize(4)
-        for i in range(4):
-            mm_weight(i)
-        ep3(0)
+        ep2(2)
         quantize(5)
+        ep1(3)
+        ep3(0)
         ep2(3)
-        ep3(1)
+        w_copy(1)
+        ep3(1, "g")
         ep3(2)
+        w_pending = None
         for s in range(2, TILES // 2):
             i, j = 2 * s, 2 * s + 1
             more = j + 2 < TILES
@@ -259,6 +274,8 @@ def tile_unmixing_residual_s10_kernel(tc, z, inv_sum, y, shade, d_words, d_scale
                 transpose(j + 2)
             mm_var(j)
             mm_mean(j)
+            w_copy(i - 1)
+            ep3(i - 1, "g")
             if j + 4 < TILES:
                 relu_scale(i + 4, "s")
             if more:
@@ -267,15 +284,18 @@ def tile_unmixing_residual_s10_kernel(tc, z, inv_sum, y, shade, d_words, d_scale
             if j + 4 < TILES:
                 relu_scale(j + 4, "s")
             ep1(i)
-            ep3(i - 1)
-            ep2(i)
             if more:
                 quantize(i + 2)
-            ep1(j)
+            ep2(i)
             if more:
                 quantize(j + 2)
-            ep2(j)
+            ep1(j)
             mm_weight(i)
             mm_weight(j)
-            ep3(i)
+            if i >= TILES - 4:
+                w_copy(i)
+                ep3(i, "g")
+            else:
+                ep3(i)
+            ep2(j)
         ep3(TILES - 1)

@@ -178,20 +178,18 @@ def tile_unmixing_residual_s10_kernel(tc, z, inv_sum, y, shade, d_words, d_scale
             nc.vector.tensor_tensor(out=resid[:], in0=t1[i][:], in1=mean[i][:], op=ALU.subtract)
             t2[i] = resid
 
-        def w_copy(i):
-            weight_sb = work.tile([P, N], F32, name="weight_sb")
-            nc.scalar.copy(out=weight_sb[:], in_=weight[i][:])
-            weight[i] = weight_sb
-
-        def ep3(i, engine="v"):
+        def ep3(i):
             if i % 2 == 0:
                 pair = work.tile([P, 2, N], F32, name="pair")
                 res[i // 2] = pair
             dst = res[i // 2]
-            (nc.gpsimd if engine == "g" else nc.vector).tensor_tensor(out=dst[:, i % 2, :], in0=t2[i][:], in1=weight[i][:], op=ALU.mult)
-            if i >= TILES - 2:
-                nc.sync.dma_start(out=out_rows[:, i, :], in_=dst[:, i % 2, :])
-            elif i % 2 == 1:
+            pieces = 2 if i == TILES - 1 else 1
+            for h in range(pieces):
+                cols = slice(h * N // pieces, (h + 1) * N // pieces)
+                nc.vector.tensor_tensor(out=dst[:, i % 2, cols], in0=t2[i][:, cols], in1=weight[i][:, cols], op=ALU.mult)
+                if i >= TILES - 2:
+                    nc.sync.dma_start(out=out_rows[:, i, cols], in_=dst[:, i % 2, cols])
+            if i % 2 == 1 and i < TILES - 2:
                 nc.sync.dma_start(out=out_rows[:, i - 1:i + 1, :], in_=dst[:])
 
         def c_group(g, engine):
@@ -260,10 +258,7 @@ def tile_unmixing_residual_s10_kernel(tc, z, inv_sum, y, shade, d_words, d_scale
         ep1(3)
         ep3(0)
         ep2(3)
-        w_copy(1)
-        ep3(1, "g")
-        ep3(2)
-        w_pending = None
+        ep3(1)
         for s in range(2, TILES // 2):
             i, j = 2 * s, 2 * s + 1
             more = j + 2 < TILES
@@ -274,8 +269,6 @@ def tile_unmixing_residual_s10_kernel(tc, z, inv_sum, y, shade, d_words, d_scale
                 transpose(j + 2)
             mm_var(j)
             mm_mean(j)
-            w_copy(i - 1)
-            ep3(i - 1, "g")
             if j + 4 < TILES:
                 relu_scale(i + 4, "s")
             if more:
@@ -283,19 +276,17 @@ def tile_unmixing_residual_s10_kernel(tc, z, inv_sum, y, shade, d_words, d_scale
                 group(j + 2, "s")
             if j + 4 < TILES:
                 relu_scale(j + 4, "s")
+            ep3(i - 2)
             ep1(i)
-            if more:
-                quantize(i + 2)
+            ep3(i - 1)
             ep2(i)
             if more:
-                quantize(j + 2)
+                quantize(i + 2)
             ep1(j)
+            if more:
+                quantize(j + 2)
+            ep2(j)
             mm_weight(i)
             mm_weight(j)
-            if i >= TILES - 4:
-                w_copy(i)
-                ep3(i, "g")
-            else:
-                ep3(i)
-            ep2(j)
+        ep3(TILES - 2)
         ep3(TILES - 1)

@@ -81,18 +81,18 @@ def tile_unmixing_residual_s10_kernel(tc, z, inv_sum, y, shade, d_words, d_scale
         nc.vector.memset(e_plane[:].rearrange("p g n -> p (g n)").bitcast(I32), 0)
         nc.vector.memset(warm[:], 0.0)
         make_identity(nc, ident[:])
-        nc.gpsimd.dma_start(out=shade_bf[:], in_=shade.rearrange("(p i) o -> p (i o)", i=TILES))
+        load_scales(nc.gpsimd, e_plane, e_scales)
         load_z(0, 1)
         nc.sync.dma_start(out=inv_bf[:], in_=inv_sum.rearrange("(p i) o -> p (i o)", i=TILES))
         load_scales(nc.sync, d_plane, d_scales)
         load_d()
         load_z(1, 1)
-        load_e()
-        load_scales(nc.sync, e_plane, e_scales)
         load_z(2, 2)
+        nc.sync.dma_start(out=shade_bf[:], in_=shade.rearrange("(p i) o -> p (i o)", i=TILES))
         load_y(0, 2)
         load_c(0)
         load_c(1)
+        load_e()
         load_z(4, 2)
         load_y(2, 2)
         load_z(6, 2)
@@ -106,37 +106,43 @@ def tile_unmixing_residual_s10_kernel(tc, z, inv_sum, y, shade, d_words, d_scale
         a, grouped, codes, planes, xt = {}, {}, {}, {}, {}
         var, mean, weight, t1, t2, res = {}, {}, {}, {}, {}, {}
 
-        def relu_scale(i, engine):
+        def relu_scale(i, engine, parts=1):
             act = work.tile([P, K], BF16, name="act", align_bytes=64)
-            src = z_sb[:, i, :].rearrange("p (q u e) -> p u q e", u=2, e=2)
-            dst = act[:].rearrange("p (u q e) -> p u q e", u=2, e=2)
-            if engine == "v":
-                nc.vector.tensor_scalar(out=dst, in0=src, scalar1=0.0, scalar2=inv_bf[:, i:i + 1], op0=ALU.max, op1=ALU.mult)
-            else:
-                nc.scalar.activation(out=dst, in_=src, func=ACT.Relu, scale=inv_col[:, i:i + 1])
+            w = K // parts
+            for h in range(parts):
+                src = z_sb[:, i, h * w:(h + 1) * w].rearrange("p (q u e) -> p u q e", u=2, e=2)
+                dst = act[:, h * w:(h + 1) * w].rearrange("p (u q e) -> p u q e", u=2, e=2)
+                if engine == "v":
+                    nc.vector.tensor_scalar(out=dst, in0=src, scalar1=0.0, scalar2=inv_bf[:, i:i + 1], op0=ALU.max, op1=ALU.mult)
+                else:
+                    nc.scalar.activation(out=dst, in_=src, func=ACT.Relu, scale=inv_col[:, i:i + 1])
             a[i] = act
 
-        def transpose(i):
+        def transpose(i, parts=1):
             turned = psum.tile([P, 2, 2 * P], F32, name="turned")
             words = a[i][:].bitcast(F32)
             for b in range(4):
-                nc.tensor.transpose(turned[:, b // 2, (b % 2) * P:(b % 2 + 1) * P], words[:, b * P:(b + 1) * P], ident[:])
+                u, g = (b // 2, b % 2) if parts == 1 else (b % 2, b // 2)
+                nc.tensor.transpose(turned[:, u, g * P:(g + 1) * P], words[:, b * P:(b + 1) * P], ident[:])
             xt[i] = turned
 
-        def group(i, engine):
+        def group(i, engine, parts=1):
             grp = work.tile([P, K], BF16, name="grp", align_bytes=64)
-            dst = grp[:].bitcast(F32).rearrange("p (x u) -> p x u", u=2)
-            src = xt[i][:].rearrange("p u x -> p x u")
-            if engine == "v":
-                nc.vector.tensor_copy(out=dst, in_=src)
-            else:
+            w = K // parts
+            for h in range(parts):
+                dst = grp[:, h * w:(h + 1) * w].bitcast(F32).rearrange("p (x u) -> p x u", u=2)
+                src = xt[i][:, :, h * w // 4:(h + 1) * w // 4].rearrange("p u x -> p x u")
                 nc.scalar.copy(out=dst, in_=src)
             grouped[i] = grp
 
-        def quantize(i):
+        def quantize(i, parts=1):
             code = work.tile([P, PASSES * P], U32, name="code", align_bytes=64)
             plane = work.tile([P, PASSES * P], U8, name="plane", align_bytes=64)
-            nc.vector.quantize_mx(out=code[:].bitcast(E4M3X4), scales=plane[:], in_=grouped[i][:])
+            w = K // parts
+            for h in range(parts):
+                words = slice(h * w // 4, (h + 1) * w // 4)
+                nc.vector.quantize_mx(
+                    out=code[:, words].bitcast(E4M3X4), scales=plane[:, words], in_=grouped[i][:, h * w:(h + 1) * w])
             codes[i], planes[i] = code, plane
 
         def product(i, acc, rhs, rhs_plane):
@@ -211,54 +217,56 @@ def tile_unmixing_residual_s10_kernel(tc, z, inv_sum, y, shade, d_words, d_scale
         transpose(0)
         transpose(1)
         group(0, "s")
-        quantize(0)
         group(1, "s")
-        quantize(1)
-        nc.vector.tensor_scalar(out=neg_shade[:], in0=shade_bf[:], scalar1=-1.0, scalar2=None, op0=ALU.mult)
-        relu_scale(2, "v")
-        relu_scale(3, "v")
+        quantize(0)
         mm_var(0)
-        mm_mean(0)
+        relu_scale(2, "s")
+        relu_scale(3, "v")
         transpose(2)
         transpose(3)
+        quantize(1)
+        nc.vector.tensor_scalar(out=neg_shade[:], in0=shade_bf[:], scalar1=-1.0, scalar2=None, op0=ALU.mult)
         mm_var(1)
-        mm_mean(1)
+        ep1(0)
         group(2, "s")
         group(3, "s")
-        ep1(0)
-        quantize(2)
-        ep2(0)
-        quantize(3)
-        ep1(1)
         c_group(0, "s")
         c_group(1, "s")
         c_group(0, "v")
-        ep2(1)
-        relu_scale(4, "v")
-        relu_scale(5, "v")
-        c_group(1, "v")
-        c_quantize(0)
-        c_quantize(1)
+        quantize(2)
+        quantize(3)
         mm_var(2)
-        mm_mean(2)
+        c_group(1, "v")
+        ep1(1)
+        mm_mean(0)
+        mm_mean(1)
         mm_var(3)
-        mm_mean(3)
+        c_quantize(0)
+        relu_scale(4, "s")
+        relu_scale(5, "v")
+        c_quantize(1)
+        ep1(2)
+        ep2(0)
+        mm_weight(0)
+        mm_weight(1)
         transpose(4)
         transpose(5)
-        for i in range(4):
-            mm_weight(i)
-        ep1(2)
+        mm_mean(2)
+        ep2(1)
+        ep3(0)
+        ep1(3)
+        mm_mean(3)
         group(4, "s")
         group(5, "s")
         relu_scale(6, "s")
         relu_scale(7, "s")
-        quantize(4)
         ep2(2)
-        quantize(5)
-        ep1(3)
-        ep3(0)
-        ep2(3)
+        quantize(4)
         ep3(1)
+        ep2(3)
+        quantize(5)
+        mm_weight(2)
+        mm_weight(3)
         for s in range(2, TILES // 2):
             i, j = 2 * s, 2 * s + 1
             more = j + 2 < TILES

@@ -7,6 +7,7 @@ M, K, N = 2048, 1024, 512
 P = 128
 TILES = M // P
 PASSES = K // 512
+C_SPLIT = N // 2
 
 FLOPS = 3 * 2 * M * K * N
 
@@ -20,10 +21,10 @@ E2M1X4 = mybir.dt.float4_e2m1fn_x4
 ALU = mybir.AluOpType
 ACT = mybir.ActivationFunctionType
 
-C_SPLIT = 256
 
-
-def tile_unmixing_residual_s10_kernel(tc, z, inv_sum, y, shade, d_words, d_scales, e_words, e_scales, c, out):
+def tile_unmixing_residual_s10_kernel(
+    tc, z, inv_sum, y, shade, d_words, d_scales, e_words, e_scales, c, out
+):
     nc = tc.nc
     z_rows = z.rearrange("(p i) k -> p i k", i=TILES)
     y_rows = y.rearrange("(p i) n -> p i n", i=TILES)
@@ -32,17 +33,17 @@ def tile_unmixing_residual_s10_kernel(tc, z, inv_sum, y, shade, d_words, d_scale
 
     with ExitStack() as ctx:
         keep = ctx.enter_context(tc.tile_pool(name="keep", bufs=1))
-        work = ctx.enter_context(tc.tile_pool(name="work", bufs=4))
+        work = ctx.enter_context(tc.tile_pool(name="work", bufs=6))
         psum = ctx.enter_context(tc.psum_pool(name="psum", bufs=2))
 
         z_sb = keep.tile([P, TILES, K], BF16, name="z_sb", align_bytes=64)
         y_sb = keep.tile([P, TILES, N], BF16, name="y_sb", align_bytes=64)
         inv_bf = keep.tile([P, TILES], BF16, name="inv_bf")
         shade_bf = keep.tile([P, TILES], BF16, name="shade_bf")
-        inv_col = keep.tile([P, TILES], F32, name="inv_col")
+        inv_f32 = keep.tile([P, TILES], F32, name="inv_f32")
         neg_shade = keep.tile([P, TILES], F32, name="neg_shade")
         ident = keep.tile([P, P], F32, name="ident")
-        warm = keep.tile([P, 16], F32, name="warm")
+        scratch = keep.tile([P, 16], F32, name="scratch")
         d_codes = keep.tile([P, PASSES, 2 * N], U8, name="d_codes", align_bytes=64)
         e_codes = keep.tile([P, PASSES, N], U32, name="e_codes", align_bytes=64)
         c_codes = keep.tile([P, PASSES, N], U32, name="c_codes", align_bytes=64)
@@ -60,39 +61,30 @@ def tile_unmixing_residual_s10_kernel(tc, z, inv_sum, y, shade, d_words, d_scale
         def load_y(first, count):
             nc.sync.dma_start(out=y_sb[:, first:first + count, :], in_=y_rows[:, first:first + count, :])
 
-        def load_scales(engine, plane, scales):
-            words = scales.bitcast(I32).rearrange("g (q r) n -> r q g n", r=4)
+        def load_scales(queue, plane, scales):
+            rows = scales.bitcast(I32).rearrange("g (q r) n -> r q g n", r=4)
             for r in range(4):
-                engine.dma_start(out=plane[r:P:32, :, :].bitcast(I32), in_=words[r])
-
-        def load_d():
-            nc.sync.dma_start(out=d_codes[:].bitcast(I32), in_=d_words.bitcast(I32).rearrange("g p w -> p g w"))
-
-        def load_e():
-            nc.sync.dma_start(
-                out=e_codes[:].bitcast(I32),
-                in_=e_words.rearrange("g p n t -> g p (n t)").bitcast(I32).rearrange("g p w -> p g w"),
-            )
-
-        def load_c(g):
-            nc.sync.dma_start(out=c_raw[:, g, :, :], in_=c_rows[g])
+                queue.dma_start(out=plane[r:P:32, :, :].bitcast(I32), in_=rows[r])
 
         nc.vector.memset(d_plane[:].rearrange("p g n -> p (g n)").bitcast(I32), 0)
         nc.vector.memset(e_plane[:].rearrange("p g n -> p (g n)").bitcast(I32), 0)
-        nc.vector.memset(warm[:], 0.0)
+        nc.vector.memset(scratch[:], 0.0)
         make_identity(nc, ident[:])
         load_scales(nc.gpsimd, e_plane, e_scales)
         load_z(0, 1)
         nc.sync.dma_start(out=inv_bf[:], in_=inv_sum.rearrange("(p i) o -> p (i o)", i=TILES))
         load_scales(nc.sync, d_plane, d_scales)
-        load_d()
         load_z(1, 1)
+        nc.sync.dma_start(out=d_codes[:].bitcast(I32), in_=d_words.bitcast(I32).rearrange("g p w -> p g w"))
         load_z(2, 2)
         nc.sync.dma_start(out=shade_bf[:], in_=shade.rearrange("(p i) o -> p (i o)", i=TILES))
         load_y(0, 2)
-        load_c(0)
-        load_c(1)
-        load_e()
+        for g in range(PASSES):
+            nc.sync.dma_start(out=c_raw[:, g, :, :], in_=c_rows[g])
+        nc.sync.dma_start(
+            out=e_codes[:].bitcast(I32),
+            in_=e_words.rearrange("g p n t -> g p (n t)").bitcast(I32).rearrange("g p w -> p g w"),
+        )
         load_z(4, 2)
         load_y(2, 2)
         load_z(6, 2)
@@ -101,200 +93,215 @@ def tile_unmixing_residual_s10_kernel(tc, z, inv_sum, y, shade, d_words, d_scale
             load_z(first, 2)
             load_y(first, 4)
             load_z(first + 2, 2)
-        nc.scalar.activation(out=warm[:, 0:1], in_=warm[:, 1:2], func=ACT.Relu)
+        nc.scalar.activation(out=scratch[:, 0:1], in_=scratch[:, 1:2], func=ACT.Relu)
 
-        a, grouped, codes, planes, xt = {}, {}, {}, {}, {}
-        var, mean, weight, t1, t2, res = {}, {}, {}, {}, {}, {}
+        a_words, turned_words, a_grouped, a_codes, a_planes = {}, {}, {}, {}, {}
 
         def relu_scale(i, engine, parts=1):
             act = work.tile([P, K], BF16, name="act", align_bytes=64)
-            w = K // parts
+            width = K // parts
             for h in range(parts):
-                src = z_sb[:, i, h * w:(h + 1) * w].rearrange("p (q u e) -> p u q e", u=2, e=2)
-                dst = act[:, h * w:(h + 1) * w].rearrange("p (u q e) -> p u q e", u=2, e=2)
-                if engine == "v":
-                    nc.vector.tensor_scalar(out=dst, in0=src, scalar1=0.0, scalar2=inv_bf[:, i:i + 1], op0=ALU.max, op1=ALU.mult)
+                cols = slice(h * width, (h + 1) * width)
+                src = z_sb[:, i, cols].rearrange("p (q u e) -> p u q e", u=2, e=2)
+                dst = act[:, cols].rearrange("p (u q e) -> p u q e", u=2, e=2)
+                if engine == "vector":
+                    nc.vector.tensor_scalar(
+                        out=dst, in0=src, scalar1=0.0, scalar2=inv_bf[:, i:i + 1], op0=ALU.max, op1=ALU.mult)
                 else:
-                    nc.scalar.activation(out=dst, in_=src, func=ACT.Relu, scale=inv_col[:, i:i + 1])
-            a[i] = act
+                    nc.scalar.activation(out=dst, in_=src, func=ACT.Relu, scale=inv_f32[:, i:i + 1])
+            a_words[i] = act
 
         def transpose(i, parts=1):
-            turned = psum.tile([P, 2, 2 * P], F32, name="turned")
-            words = a[i][:].bitcast(F32)
-            for b in range(4):
-                u, g = (b // 2, b % 2) if parts == 1 else (b % 2, b // 2)
+            turned = psum.tile([P, 2, PASSES * P], F32, name="turned")
+            words = a_words[i][:].bitcast(F32)
+            for b in range(2 * PASSES):
+                u, g = divmod(b, PASSES) if parts == 1 else (b % 2, b // 2)
                 nc.tensor.transpose(turned[:, u, g * P:(g + 1) * P], words[:, b * P:(b + 1) * P], ident[:])
-            xt[i] = turned
+            turned_words[i] = turned
 
-        def group(i, engine, parts=1):
-            grp = work.tile([P, K], BF16, name="grp", align_bytes=64)
-            w = K // parts
+        def interleave(i, parts=1):
+            grouped = work.tile([P, K], BF16, name="grouped", align_bytes=64)
+            width = K // parts
             for h in range(parts):
-                dst = grp[:, h * w:(h + 1) * w].bitcast(F32).rearrange("p (x u) -> p x u", u=2)
-                src = xt[i][:, :, h * w // 4:(h + 1) * w // 4].rearrange("p u x -> p x u")
-                nc.scalar.copy(out=dst, in_=src)
-            grouped[i] = grp
+                nc.scalar.copy(
+                    out=grouped[:, h * width:(h + 1) * width].bitcast(F32).rearrange("p (x u) -> p x u", u=2),
+                    in_=turned_words[i][:, :, h * width // 4:(h + 1) * width // 4].rearrange("p u x -> p x u"),
+                )
+            a_grouped[i] = grouped
 
         def quantize(i, parts=1):
-            code = work.tile([P, PASSES * P], U32, name="code", align_bytes=64)
+            codes = work.tile([P, PASSES * P], U32, name="codes", align_bytes=64)
             plane = work.tile([P, PASSES * P], U8, name="plane", align_bytes=64)
-            w = K // parts
+            width = K // parts
             for h in range(parts):
-                words = slice(h * w // 4, (h + 1) * w // 4)
+                cols = slice(h * width // 4, (h + 1) * width // 4)
                 nc.vector.quantize_mx(
-                    out=code[:, words].bitcast(E4M3X4), scales=plane[:, words], in_=grouped[i][:, h * w:(h + 1) * w])
-            codes[i], planes[i] = code, plane
-
-        def product(i, acc, rhs, rhs_plane):
-            for g in range(PASSES):
-                cols = slice(g * P, (g + 1) * P)
-                nc.tensor.matmul_mx(
-                    out=acc[:],
-                    lhsT=codes[i][:, cols].bitcast(E4M3X4),
-                    lhsT_scale=planes[i][:, cols],
-                    rhs=rhs(g),
-                    rhs_scale=rhs_plane[:, g, :],
-                    start=(g == 0),
-                    stop=(g == PASSES - 1),
+                    out=codes[:, cols].bitcast(E4M3X4),
+                    scales=plane[:, cols],
+                    in_=a_grouped[i][:, h * width:(h + 1) * width],
                 )
+            a_codes[i], a_planes[i] = codes, plane
 
-        def mm_var(i):
-            var_ps = psum.tile([P, N], F32, name="var_ps")
-            product(i, var_ps, lambda g: d_codes[:, g, :].bitcast(E2M1X4), d_plane)
-            var[i] = var_ps
-
-        def mm_mean(i):
-            mean_ps = psum.tile([P, N], F32, name="mean_ps")
-            product(i, mean_ps, lambda g: e_codes[:, g, :].bitcast(E4M3X4), e_plane)
-            mean[i] = mean_ps
-
-        def mm_weight(i):
-            weight_ps = psum.tile([P, N], F32, name="weight_ps")
-            product(i, weight_ps, lambda g: c_codes[:, g, :].bitcast(E4M3X4), c_plane)
-            weight[i] = weight_ps
-
-        def ep1(i):
-            part = work.tile([P, N], F32, name="part")
-            nc.vector.scalar_tensor_tensor(
-                out=part[:], in0=var[i][:], scalar=neg_shade[:, i:i + 1], in1=y_sb[:, i, :], op0=ALU.mult, op1=ALU.add)
-            t1[i] = part
-
-        def ep2(i):
-            resid = work.tile([P, N], F32, name="resid")
-            nc.vector.tensor_tensor(out=resid[:], in0=t1[i][:], in1=mean[i][:], op=ALU.subtract)
-            t2[i] = resid
-
-        def ep3(i):
-            if i % 2 == 0:
-                pair = work.tile([P, 2, N], F32, name="pair")
-                res[i // 2] = pair
-            dst = res[i // 2]
-            pieces = 2 if i == TILES - 1 else 1
-            for h in range(pieces):
-                cols = slice(h * N // pieces, (h + 1) * N // pieces)
-                nc.vector.tensor_tensor(out=dst[:, i % 2, cols], in0=t2[i][:, cols], in1=weight[i][:, cols], op=ALU.mult)
-                if i >= TILES - 2:
-                    nc.sync.dma_start(out=out_rows[:, i, cols], in_=dst[:, i % 2, cols])
-            if i % 2 == 1 and i < TILES - 2:
-                nc.sync.dma_start(out=out_rows[:, i - 1:i + 1, :], in_=dst[:])
-
-        def c_group(g, engine):
-            cols = slice(0, C_SPLIT) if engine == "v" else slice(C_SPLIT, N)
-            src = c_raw[:, g, :, cols].rearrange("p j n -> p n j")
-            dst = c_grouped[:, g, cols, :]
-            if engine == "v":
+        def interleave_c(g, engine):
+            cols = slice(0, C_SPLIT) if engine == "vector" else slice(C_SPLIT, N)
+            src = c_raw[:, g, :, cols].rearrange("p j (n i) -> p n j i", i=4)
+            dst = c_grouped[:, g, cols, :].rearrange("p (n i) j -> p n j i", i=4)
+            if engine == "vector":
                 nc.vector.tensor_copy(out=dst, in_=src)
             else:
                 nc.scalar.copy(out=dst, in_=src)
 
-        def c_quantize(g):
+        def quantize_c(g):
             nc.vector.quantize_mx(
-                out=c_codes[:, g, :].bitcast(E4M3X4), scales=c_plane[:, g, :], in_=c_grouped[:, g, :, :].rearrange("p n j -> p (n j)"))
+                out=c_codes[:, g, :].bitcast(E4M3X4),
+                scales=c_plane[:, g, :],
+                in_=c_grouped[:, g, :, :].rearrange("p n j -> p (n j)"),
+            )
 
-        relu_scale(0, "v")
-        nc.vector.tensor_copy(out=inv_col[:], in_=inv_bf[:])
-        relu_scale(1, "v")
-        transpose(0)
+        var, mean, weight = {}, {}, {}
+
+        def product(i, acc, library, library_plane):
+            for g in range(PASSES):
+                pixels = slice(g * P, (g + 1) * P)
+                nc.tensor.matmul_mx(
+                    out=acc[:],
+                    lhsT=a_codes[i][:, pixels].bitcast(E4M3X4),
+                    lhsT_scale=a_planes[i][:, pixels],
+                    rhs=library(g),
+                    rhs_scale=library_plane[:, g, :],
+                    start=(g == 0),
+                    stop=(g == PASSES - 1),
+                )
+
+        def matmul_var(i):
+            var_ps = psum.tile([P, N], F32, name="var_ps")
+            product(i, var_ps, lambda g: d_codes[:, g, :].bitcast(E2M1X4), d_plane)
+            var[i] = var_ps
+
+        def matmul_mean(i):
+            mean_ps = psum.tile([P, N], F32, name="mean_ps")
+            product(i, mean_ps, lambda g: e_codes[:, g, :].bitcast(E4M3X4), e_plane)
+            mean[i] = mean_ps
+
+        def matmul_weight(i):
+            weight_ps = psum.tile([P, N], F32, name="weight_ps")
+            product(i, weight_ps, lambda g: c_codes[:, g, :].bitcast(E4M3X4), c_plane)
+            weight[i] = weight_ps
+
+        shaded, residual, result = {}, {}, {}
+
+        def subtract_var(i):
+            diff = work.tile([P, N], F32, name="diff")
+            nc.vector.scalar_tensor_tensor(
+                out=diff[:], in0=var[i][:], scalar=neg_shade[:, i:i + 1], in1=y_sb[:, i, :], op0=ALU.mult, op1=ALU.add)
+            shaded[i] = diff
+
+        def subtract_mean(i):
+            resid = work.tile([P, N], F32, name="resid")
+            nc.vector.tensor_tensor(out=resid[:], in0=shaded[i][:], in1=mean[i][:], op=ALU.subtract)
+            residual[i] = resid
+
+        def multiply_weight(i):
+            s, side = divmod(i, 2)
+            if side == 0:
+                pair = work.tile([P, 2, N], F32, name="pair")
+                result[s] = pair
+            pieces = 2 if i == TILES - 1 else 1
+            for h in range(pieces):
+                cols = slice(h * N // pieces, (h + 1) * N // pieces)
+                nc.vector.tensor_tensor(
+                    out=result[s][:, side, cols], in0=residual[i][:, cols], in1=weight[i][:, cols], op=ALU.mult)
+                if i >= TILES - 2:
+                    nc.sync.dma_start(out=out_rows[:, i, cols], in_=result[s][:, side, cols])
+            if side == 1 and i < TILES - 2:
+                nc.sync.dma_start(out=out_rows[:, i - 1:i + 1, :], in_=result[s][:])
+
+        relu_scale(0, "vector", parts=2)
+        nc.vector.tensor_copy(out=inv_f32[:], in_=inv_bf[:])
+        relu_scale(1, "vector")
+        transpose(0, parts=2)
         transpose(1)
-        group(0, "s")
-        group(1, "s")
-        quantize(0)
-        mm_var(0)
-        relu_scale(2, "s")
-        relu_scale(3, "v")
+        interleave(0, parts=2)
+        interleave(1)
+        quantize(0, parts=2)
+        relu_scale(2, "vector")
+        quantize(1)
+        relu_scale(3, "vector")
+        matmul_var(0)
         transpose(2)
         transpose(3)
-        quantize(1)
         nc.vector.tensor_scalar(out=neg_shade[:], in0=shade_bf[:], scalar1=-1.0, scalar2=None, op0=ALU.mult)
-        mm_var(1)
-        ep1(0)
-        group(2, "s")
-        group(3, "s")
-        c_group(0, "s")
-        c_group(1, "s")
-        c_group(0, "v")
+        subtract_var(0)
+        interleave(2)
+        interleave(3)
+        interleave_c(0, "scalar")
+        interleave_c(1, "scalar")
+        matmul_var(1)
         quantize(2)
+        interleave_c(0, "vector")
         quantize(3)
-        mm_var(2)
-        c_group(1, "v")
-        ep1(1)
-        mm_mean(0)
-        mm_mean(1)
-        mm_var(3)
-        c_quantize(0)
-        relu_scale(4, "s")
-        relu_scale(5, "v")
-        c_quantize(1)
-        ep1(2)
-        ep2(0)
-        mm_weight(0)
-        mm_weight(1)
+        subtract_var(1)
+        matmul_var(2)
+        matmul_var(3)
+        interleave_c(1, "vector")
+        matmul_mean(0)
+        matmul_mean(1)
+        relu_scale(4, "scalar")
+        relu_scale(5, "scalar")
+        quantize_c(0)
+        quantize_c(1)
+        subtract_mean(0)
+        subtract_mean(1)
+        matmul_weight(0)
+        matmul_weight(1)
+        subtract_var(2)
+        matmul_mean(2)
         transpose(4)
         transpose(5)
-        mm_mean(2)
-        ep2(1)
-        ep3(0)
-        ep1(3)
-        mm_mean(3)
-        group(4, "s")
-        group(5, "s")
-        relu_scale(6, "s")
-        relu_scale(7, "s")
-        ep2(2)
+        matmul_mean(3)
+        multiply_weight(0)
+        subtract_var(3)
+        subtract_mean(2)
+        interleave(4)
+        interleave(5)
+        relu_scale(6, "scalar")
+        relu_scale(7, "scalar")
+        multiply_weight(1)
         quantize(4)
-        ep3(1)
-        ep2(3)
+        subtract_mean(3)
         quantize(5)
-        mm_weight(2)
-        mm_weight(3)
-        for s in range(2, TILES // 2):
-            i, j = 2 * s, 2 * s + 1
-            more = j + 2 < TILES
-            mm_var(i)
-            mm_mean(i)
-            if more:
+        matmul_weight(2)
+        matmul_weight(3)
+
+        for i in range(4, TILES, 2):
+            j = i + 1
+            turn_next = j + 2 < TILES
+            relu_next = j + 4 < TILES
+            matmul_var(i)
+            matmul_mean(i)
+            if turn_next:
                 transpose(i + 2)
                 transpose(j + 2)
-            mm_var(j)
-            mm_mean(j)
-            if j + 4 < TILES:
-                relu_scale(i + 4, "s")
-            if more:
-                group(i + 2, "s")
-                group(j + 2, "s")
-            if j + 4 < TILES:
-                relu_scale(j + 4, "s")
-            ep3(i - 2)
-            ep1(i)
-            ep3(i - 1)
-            ep2(i)
-            if more:
+            matmul_var(j)
+            matmul_mean(j)
+            if relu_next:
+                relu_scale(i + 4, "scalar")
+            if turn_next:
+                interleave(i + 2)
+                interleave(j + 2)
+            if relu_next:
+                relu_scale(j + 4, "scalar")
+            multiply_weight(i - 2)
+            subtract_var(i)
+            multiply_weight(j - 2)
+            subtract_mean(i)
+            if turn_next:
                 quantize(i + 2)
-            ep1(j)
-            if more:
+            subtract_var(j)
+            if turn_next:
                 quantize(j + 2)
-            ep2(j)
-            mm_weight(i)
-            mm_weight(j)
-        ep3(TILES - 2)
-        ep3(TILES - 1)
+            subtract_mean(j)
+            matmul_weight(i)
+            matmul_weight(j)
+        multiply_weight(TILES - 2)
+        multiply_weight(TILES - 1)

from contextlib import ExitStack

import concourse.mybir as mybir
from concourse.masks import make_identity

M, K, N = 2048, 1024, 512
P = 128
TILES = M // P
PASSES = K // 512
C_SPLIT = N // 2

FLOPS = 3 * 2 * M * K * N

F32 = mybir.dt.float32
BF16 = mybir.dt.bfloat16
I32 = mybir.dt.int32
U32 = mybir.dt.uint32
U8 = mybir.dt.uint8
E4M3X4 = mybir.dt.float8_e4m3fn_x4
E2M1X4 = mybir.dt.float4_e2m1fn_x4
ALU = mybir.AluOpType
ACT = mybir.ActivationFunctionType


def tile_unmixing_residual_s10_kernel(
    tc, z, inv_sum, y, shade, d_words, d_scales, e_words, e_scales, c, out
):
    nc = tc.nc
    z_rows = z.rearrange("(p i) k -> p i k", i=TILES)
    y_rows = y.rearrange("(p i) n -> p i n", i=TILES)
    out_rows = out.rearrange("(p i) n -> p i n", i=TILES)
    c_rows = c.rearrange("(g p j) n -> g p j n", p=P, j=4)

    with ExitStack() as ctx:
        keep = ctx.enter_context(tc.tile_pool(name="keep", bufs=1))
        work = ctx.enter_context(tc.tile_pool(name="work", bufs=6))
        psum = ctx.enter_context(tc.psum_pool(name="psum", bufs=2))

        z_sb = keep.tile([P, TILES, K], BF16, name="z_sb", align_bytes=64)
        y_sb = keep.tile([P, TILES, N], BF16, name="y_sb", align_bytes=64)
        inv_bf = keep.tile([P, TILES], BF16, name="inv_bf")
        shade_bf = keep.tile([P, TILES], BF16, name="shade_bf")
        inv_f32 = keep.tile([P, TILES], F32, name="inv_f32")
        neg_shade = keep.tile([P, TILES], F32, name="neg_shade")
        ident = keep.tile([P, P], F32, name="ident")
        scratch = keep.tile([P, 16], F32, name="scratch")
        d_codes = keep.tile([P, PASSES, 2 * N], U8, name="d_codes", align_bytes=64)
        e_codes = keep.tile([P, PASSES, N], U32, name="e_codes", align_bytes=64)
        c_codes = keep.tile([P, PASSES, N], U32, name="c_codes", align_bytes=64)
        d_plane = keep.tile([P, PASSES, N], U8, name="d_plane", align_bytes=64)
        e_plane = keep.tile([P, PASSES, N], U8, name="e_plane", align_bytes=64)
        c_plane = keep.tile([P, PASSES, N], U8, name="c_plane", align_bytes=64)
        c_raw = keep.tile([P, PASSES, 4, N], BF16, name="c_raw", align_bytes=64)
        c_grouped = keep.tile([P, PASSES, N, 4], BF16, name="c_grouped", align_bytes=64)

        ctx.enter_context(tc.manual_schedule())

        def load_z(first, count):
            nc.sync.dma_start(out=z_sb[:, first:first + count, :], in_=z_rows[:, first:first + count, :])

        def load_y(first, count):
            nc.sync.dma_start(out=y_sb[:, first:first + count, :], in_=y_rows[:, first:first + count, :])

        def load_scales(queue, plane, scales):
            rows = scales.bitcast(I32).rearrange("g (q r) n -> r q g n", r=4)
            for r in range(4):
                queue.dma_start(out=plane[r:P:32, :, :].bitcast(I32), in_=rows[r])

        nc.vector.memset(d_plane[:].rearrange("p g n -> p (g n)").bitcast(I32), 0)
        nc.vector.memset(e_plane[:].rearrange("p g n -> p (g n)").bitcast(I32), 0)
        nc.vector.memset(scratch[:], 0.0)
        make_identity(nc, ident[:])
        load_scales(nc.gpsimd, e_plane, e_scales)
        load_z(0, 1)
        nc.sync.dma_start(out=inv_bf[:], in_=inv_sum.rearrange("(p i) o -> p (i o)", i=TILES))
        load_scales(nc.sync, d_plane, d_scales)
        load_z(1, 1)
        nc.sync.dma_start(out=d_codes[:].bitcast(I32), in_=d_words.bitcast(I32).rearrange("g p w -> p g w"))
        load_z(2, 2)
        nc.sync.dma_start(out=shade_bf[:], in_=shade.rearrange("(p i) o -> p (i o)", i=TILES))
        load_y(0, 2)
        for g in range(PASSES):
            nc.sync.dma_start(out=c_raw[:, g, :, :], in_=c_rows[g])
        nc.sync.dma_start(
            out=e_codes[:].bitcast(I32),
            in_=e_words.rearrange("g p n t -> g p (n t)").bitcast(I32).rearrange("g p w -> p g w"),
        )
        load_z(4, 2)
        load_y(2, 2)
        load_z(6, 2)
        load_y(4, 4)
        for first in range(8, TILES, 4):
            load_z(first, 2)
            load_y(first, 4)
            load_z(first + 2, 2)
        nc.scalar.activation(out=scratch[:, 0:1], in_=scratch[:, 1:2], func=ACT.Relu)

        a_words, turned_words, a_grouped, a_codes, a_planes = {}, {}, {}, {}, {}

        def relu_scale(i, engine, parts=1):
            act = work.tile([P, K], BF16, name="act", align_bytes=64)
            width = K // parts
            for h in range(parts):
                cols = slice(h * width, (h + 1) * width)
                src = z_sb[:, i, cols].rearrange("p (q u e) -> p u q e", u=2, e=2)
                dst = act[:, cols].rearrange("p (u q e) -> p u q e", u=2, e=2)
                if engine == "vector":
                    nc.vector.tensor_scalar(
                        out=dst, in0=src, scalar1=0.0, scalar2=inv_bf[:, i:i + 1], op0=ALU.max, op1=ALU.mult)
                else:
                    nc.scalar.activation(out=dst, in_=src, func=ACT.Relu, scale=inv_f32[:, i:i + 1])
            a_words[i] = act

        def transpose(i, parts=1):
            turned = psum.tile([P, 2, PASSES * P], F32, name="turned")
            words = a_words[i][:].bitcast(F32)
            for b in range(2 * PASSES):
                u, g = divmod(b, PASSES) if parts == 1 else (b % 2, b // 2)
                nc.tensor.transpose(turned[:, u, g * P:(g + 1) * P], words[:, b * P:(b + 1) * P], ident[:])
            turned_words[i] = turned

        def interleave(i, parts=1):
            grouped = work.tile([P, K], BF16, name="grouped", align_bytes=64)
            width = K // parts
            for h in range(parts):
                nc.scalar.copy(
                    out=grouped[:, h * width:(h + 1) * width].bitcast(F32).rearrange("p (x u) -> p x u", u=2),
                    in_=turned_words[i][:, :, h * width // 4:(h + 1) * width // 4].rearrange("p u x -> p x u"),
                )
            a_grouped[i] = grouped

        def quantize(i, parts=1):
            codes = work.tile([P, PASSES * P], U32, name="codes", align_bytes=64)
            plane = work.tile([P, PASSES * P], U8, name="plane", align_bytes=64)
            width = K // parts
            for h in range(parts):
                cols = slice(h * width // 4, (h + 1) * width // 4)
                nc.vector.quantize_mx(
                    out=codes[:, cols].bitcast(E4M3X4),
                    scales=plane[:, cols],
                    in_=a_grouped[i][:, h * width:(h + 1) * width],
                )
            a_codes[i], a_planes[i] = codes, plane

        def interleave_c(g, engine):
            cols = slice(0, C_SPLIT) if engine == "vector" else slice(C_SPLIT, N)
            src = c_raw[:, g, :, cols].rearrange("p j (n i) -> p n j i", i=4)
            dst = c_grouped[:, g, cols, :].rearrange("p (n i) j -> p n j i", i=4)
            if engine == "vector":
                nc.vector.tensor_copy(out=dst, in_=src)
            else:
                nc.scalar.copy(out=dst, in_=src)

        def quantize_c(g):
            nc.vector.quantize_mx(
                out=c_codes[:, g, :].bitcast(E4M3X4),
                scales=c_plane[:, g, :],
                in_=c_grouped[:, g, :, :].rearrange("p n j -> p (n j)"),
            )

        var, mean, weight = {}, {}, {}

        def product(i, acc, library, library_plane):
            for g in range(PASSES):
                pixels = slice(g * P, (g + 1) * P)
                nc.tensor.matmul_mx(
                    out=acc[:],
                    lhsT=a_codes[i][:, pixels].bitcast(E4M3X4),
                    lhsT_scale=a_planes[i][:, pixels],
                    rhs=library(g),
                    rhs_scale=library_plane[:, g, :],
                    start=(g == 0),
                    stop=(g == PASSES - 1),
                )

        def matmul_var(i):
            var_ps = psum.tile([P, N], F32, name="var_ps")
            product(i, var_ps, lambda g: d_codes[:, g, :].bitcast(E2M1X4), d_plane)
            var[i] = var_ps

        def matmul_mean(i):
            mean_ps = psum.tile([P, N], F32, name="mean_ps")
            product(i, mean_ps, lambda g: e_codes[:, g, :].bitcast(E4M3X4), e_plane)
            mean[i] = mean_ps

        def matmul_weight(i):
            weight_ps = psum.tile([P, N], F32, name="weight_ps")
            product(i, weight_ps, lambda g: c_codes[:, g, :].bitcast(E4M3X4), c_plane)
            weight[i] = weight_ps

        shaded, residual, result = {}, {}, {}

        def subtract_var(i):
            diff = work.tile([P, N], F32, name="diff")
            nc.vector.scalar_tensor_tensor(
                out=diff[:], in0=var[i][:], scalar=neg_shade[:, i:i + 1], in1=y_sb[:, i, :], op0=ALU.mult, op1=ALU.add)
            shaded[i] = diff

        def subtract_mean(i):
            resid = work.tile([P, N], F32, name="resid")
            nc.vector.tensor_tensor(out=resid[:], in0=shaded[i][:], in1=mean[i][:], op=ALU.subtract)
            residual[i] = resid

        def multiply_weight(i):
            s, side = divmod(i, 2)
            if side == 0:
                pair = work.tile([P, 2, N], F32, name="pair")
                result[s] = pair
            pieces = 2 if i == TILES - 1 else 1
            for h in range(pieces):
                cols = slice(h * N // pieces, (h + 1) * N // pieces)
                nc.vector.tensor_tensor(
                    out=result[s][:, side, cols], in0=residual[i][:, cols], in1=weight[i][:, cols], op=ALU.mult)
                if i >= TILES - 2:
                    nc.sync.dma_start(out=out_rows[:, i, cols], in_=result[s][:, side, cols])
            if side == 1 and i < TILES - 2:
                nc.sync.dma_start(out=out_rows[:, i - 1:i + 1, :], in_=result[s][:])

        relu_scale(0, "vector", parts=2)
        nc.vector.tensor_copy(out=inv_f32[:], in_=inv_bf[:])
        relu_scale(1, "vector")
        transpose(0, parts=2)
        transpose(1)
        interleave(0, parts=2)
        interleave(1)
        quantize(0, parts=2)
        relu_scale(2, "vector")
        quantize(1)
        relu_scale(3, "vector")
        matmul_var(0)
        transpose(2)
        transpose(3)
        nc.vector.tensor_scalar(out=neg_shade[:], in0=shade_bf[:], scalar1=-1.0, scalar2=None, op0=ALU.mult)
        subtract_var(0)
        interleave(2)
        interleave(3)
        interleave_c(0, "scalar")
        interleave_c(1, "scalar")
        matmul_var(1)
        quantize(2)
        interleave_c(0, "vector")
        quantize(3)
        subtract_var(1)
        matmul_var(2)
        matmul_var(3)
        interleave_c(1, "vector")
        matmul_mean(0)
        matmul_mean(1)
        relu_scale(4, "scalar")
        relu_scale(5, "scalar")
        quantize_c(0)
        quantize_c(1)
        subtract_mean(0)
        subtract_mean(1)
        matmul_weight(0)
        matmul_weight(1)
        subtract_var(2)
        matmul_mean(2)
        transpose(4)
        transpose(5)
        matmul_mean(3)
        multiply_weight(0)
        subtract_var(3)
        subtract_mean(2)
        interleave(4)
        interleave(5)
        relu_scale(6, "scalar")
        relu_scale(7, "scalar")
        multiply_weight(1)
        quantize(4)
        subtract_mean(3)
        quantize(5)
        matmul_weight(2)
        matmul_weight(3)

        for i in range(4, TILES, 2):
            j = i + 1
            turn_next = j + 2 < TILES
            relu_next = j + 4 < TILES
            matmul_var(i)
            matmul_mean(i)
            if turn_next:
                transpose(i + 2)
                transpose(j + 2)
            matmul_var(j)
            matmul_mean(j)
            if relu_next:
                relu_scale(i + 4, "scalar")
            if turn_next:
                interleave(i + 2)
                interleave(j + 2)
            if relu_next:
                relu_scale(j + 4, "scalar")
            multiply_weight(i - 2)
            subtract_var(i)
            multiply_weight(j - 2)
            subtract_mean(i)
            if turn_next:
                quantize(i + 2)
            subtract_var(j)
            if turn_next:
                quantize(j + 2)
            subtract_mean(j)
            matmul_weight(i)
            matmul_weight(j)
        multiply_weight(TILES - 2)
        multiply_weight(TILES - 1)
